import numpy as np
import ml_dtypes

BF16 = ml_dtypes.bfloat16


def bf(x):
    return np.asarray(x, np.float32).astype(BF16)


def f32(x):
    return np.asarray(x, np.float32)


def f64(x):
    return np.asarray(x).astype(np.float64)


def striped(idx):
    return np.tile(idx.reshape(-1, 16).T, (8, 1))


def rows(idx, k):
    return np.tile(idx, (k, 1))


def look(tab, idx):
    return np.take_along_axis(f64(tab), rows(idx, len(tab)), axis=1)


K, S, D, V, N, M = 256, 2048, 2, 1024, 2048, 128


def setup_inputs():
    return {"tab": f32(np.random.standard_normal((K, S))), "x0": f32(1.0 * np.random.standard_normal((K, V))), "w": bf(np.random.standard_normal((K, M)) / np.sqrt(K)), "b": f32(0.5 * np.random.standard_normal((M, 1))), "offs": striped(np.random.permutation(S)[:N])}


def reference(tab, x0, w, b, offs):
    idx = offs[:16].T.reshape(-1)
    m = f64(x0)
    for d in range(D):
        m = np.maximum(m, look(tab, idx[d * V:(d + 1) * V]))
    x = m + np.log(np.exp(f64(x0) - m) + sum(np.exp(look(tab, idx[d * V:(d + 1) * V]) - m) for d in range(D)))
    return np.maximum(f64(w).T @ x + f64(b), 0.0)

@@ -1,0 +1,77 @@
+import concourse.mybir as mybir
+
+F32, BF16, U16 = mybir.dt.float32, mybir.dt.bfloat16, mybir.dt.uint16
+Alu = mybir.AluOpType
+Act = mybir.ActivationFunctionType
+
+P = 128
+K, S, D, V, M = 256, 2048, 2, 1024, 128
+R = K // P
+C = 512
+FLOPS = 2 * K * M * V
+
+
+def tile_lookup_lse_relu_kernel(tc, tab, x0, w, b, offs, out):
+    nc = tc.nc
+    with (
+        tc.tile_pool(name="held", bufs=1) as held,
+        tc.tile_pool(name="work", bufs=2) as work,
+        tc.psum_pool(name="psum", bufs=2) as psum,
+    ):
+        offsets = held.tile([P, D * V // 16], U16, name="offsets")
+        nc.sync.dma_start(offsets[:], offs)
+
+        tables = [held.tile([P, S], F32, name=f"table{r}") for r in range(R)]
+        own = {(r, j): held.tile([P, C], F32, name=f"own{r}_{j}") for j in range(0, V, C) for r in range(R)}
+        weights = held.tile([P, R * M], BF16, name="weights")
+        bias = held.tile([P, 1], F32, name="bias")
+        for j in range(0, V, C):
+            for r in range(R):
+                rows = slice(r * P, (r + 1) * P)
+                if j == 0:
+                    nc.sync.dma_start(tables[r][:], tab[rows, :])
+                nc.sync.dma_start(own[r, j][:], x0[rows, j : j + C])
+        for r in range(R):
+            nc.scalar.dma_start(weights[:, r * M : (r + 1) * M], w[r * P : (r + 1) * P, :])
+        nc.scalar.dma_start(bias[:], b)
+
+        def picked(r, d, j):
+            first = (d * V + j) // 16
+            return tables[r][:].indirect(offsets[:, first : first + C // 16])
+
+        def exponentials(r, j):
+            h0 = work.tile([P, C], F32, name="h0")
+            h = work.tile([P, C], F32, name="h")
+            nc.vector.tensor_tensor(h0[:], picked(r, 0, j), own[r, j][:], Alu.max)
+            nc.vector.tensor_tensor(h[:], picked(r, 1, j), h0[:], Alu.max)
+            diffs = [work.tile([P, C], F32, name=f"diff{t}") for t in range(1 + D)]
+            exps = [work.tile([P, C], F32, name=f"exp{t}") for t in range(1 + D)]
+            nc.vector.tensor_tensor(diffs[0][:], own[r, j][:], h[:], Alu.subtract)
+            for d in range(D):
+                nc.vector.tensor_tensor(diffs[1 + d][:], picked(r, d, j), h[:], Alu.subtract)
+            for t in range(1 + D):
+                nc.scalar.activation(exps[t][:], diffs[t][:], Act.Exp)
+            return h, exps
+
+        def smooth_maximum(h, exps):
+            sum0 = work.tile([P, C], F32, name="sum0")
+            sum1 = work.tile([P, C], F32, name="sum1")
+            nc.vector.tensor_tensor(sum0[:], exps[0][:], exps[1][:], Alu.add)
+            nc.vector.tensor_tensor(sum1[:], sum0[:], exps[2][:], Alu.add)
+            log = work.tile([P, C], F32, name="log")
+            nc.scalar.activation(log[:], sum1[:], Act.Ln)
+            x = work.tile([P, C], BF16, name="x")
+            nc.vector.tensor_tensor(x[:], h[:], log[:], Alu.add)
+            return x
+
+        for j in range(0, V, C):
+            product = psum.tile([M, C], F32, name="product")
+            for r in range(R):
+                h, exps = exponentials(r, j)
+                x = smooth_maximum(h, exps)
+                nc.tensor.matmul(
+                    product[:], weights[:, r * M : (r + 1) * M], x[:], start=(r == 0), stop=(r == R - 1)
+                )
+            result = work.tile([M, C], F32, name="result")
+            nc.scalar.activation(result[:], product[:], Act.Relu, bias=bias[:])
+            nc.sync.dma_start(out[:, j : j + C], result[:])

@@ -1,4 +1,5 @@
 import concourse.mybir as mybir
+from concourse.masks import make_identity
 
 F32, BF16, U16 = mybir.dt.float32, mybir.dt.bfloat16, mybir.dt.uint16
 Alu = mybir.AluOpType
@@ -25,6 +26,8 @@ def tile_lookup_lse_relu_kernel(tc, tab, x0, w, b, offs, out):
         own = {(r, j): held.tile([P, C], F32, name=f"own{r}_{j}") for j in range(0, V, C) for r in range(R)}
         weights = held.tile([P, R * M], BF16, name="weights")
         bias = held.tile([P, 1], F32, name="bias")
+        identity = held.tile([P, P], F32, name="identity")
+        make_identity(nc, identity[:])
         for j in range(0, V, C):
             for r in range(R):
                 rows = slice(r * P, (r + 1) * P)
@@ -39,36 +42,31 @@ def tile_lookup_lse_relu_kernel(tc, tab, x0, w, b, offs, out):
             first = (d * V + j) // 16
             return tables[r][:].indirect(offsets[:, first : first + C // 16])
 
-        def exponentials(r, j):
-            h0 = work.tile([P, C], F32, name="h0")
-            h = work.tile([P, C], F32, name="h")
-            nc.vector.tensor_tensor(h0[:], picked(r, 0, j), own[r, j][:], Alu.max)
-            nc.vector.tensor_tensor(h[:], picked(r, 1, j), h0[:], Alu.max)
-            diffs = [work.tile([P, C], F32, name=f"diff{t}") for t in range(1 + D)]
-            exps = [work.tile([P, C], F32, name=f"exp{t}") for t in range(1 + D)]
-            nc.vector.tensor_tensor(diffs[0][:], own[r, j][:], h[:], Alu.subtract)
-            for d in range(D):
-                nc.vector.tensor_tensor(diffs[1 + d][:], picked(r, d, j), h[:], Alu.subtract)
-            for t in range(1 + D):
-                nc.scalar.activation(exps[t][:], diffs[t][:], Act.Exp)
-            return h, exps
-
-        def smooth_maximum(h, exps):
-            sum0 = work.tile([P, C], F32, name="sum0")
-            sum1 = work.tile([P, C], F32, name="sum1")
-            nc.vector.tensor_tensor(sum0[:], exps[0][:], exps[1][:], Alu.add)
-            nc.vector.tensor_tensor(sum1[:], sum0[:], exps[2][:], Alu.add)
-            log = work.tile([P, C], F32, name="log")
-            nc.scalar.activation(log[:], sum1[:], Act.Ln)
-            x = work.tile([P, C], BF16, name="x")
-            nc.vector.tensor_tensor(x[:], h[:], log[:], Alu.add)
-            return x
-
         for j in range(0, V, C):
+            h = [work.tile([P, C], F32, name=f"h{r}") for r in range(R)]
+            for r in range(R):
+                part = work.tile([P, C], F32, name=f"part{r}")
+                nc.vector.tensor_tensor(part[:], picked(r, 0, j), own[r, j][:], Alu.max)
+                nc.vector.tensor_tensor(h[r][:], picked(r, 1, j), part[:], Alu.max)
+
+            sums = [psum.tile([P, C], F32, name=f"sum{r}") for r in range(R)]
+            for t in range(1 + D):
+                for r in range(R):
+                    diff = work.tile([P, C], F32, name=f"diff{r}")
+                    if t == 0:
+                        nc.vector.tensor_tensor(diff[:], own[r, j][:], h[r][:], Alu.subtract)
+                    else:
+                        nc.vector.tensor_tensor(diff[:], picked(r, t - 1, j), h[r][:], Alu.subtract)
+                    power = work.tile([P, C], F32, name=f"power{r}")
+                    nc.scalar.activation(power[:], diff[:], Act.Exp)
+                    nc.tensor.matmul(sums[r][:], identity[:], power[:], start=(t == 0), stop=(t == D))
+
             product = psum.tile([M, C], F32, name="product")
             for r in range(R):
-                h, exps = exponentials(r, j)
-                x = smooth_maximum(h, exps)
+                log = work.tile([P, C], F32, name=f"log{r}")
+                nc.scalar.activation(log[:], sums[r][:], Act.Ln)
+                x = work.tile([P, C], BF16, name=f"x{r}")
+                nc.vector.tensor_tensor(x[:], h[r][:], log[:], Alu.add)
                 nc.tensor.matmul(
                     product[:], weights[:, r * M : (r + 1) * M], x[:], start=(r == 0), stop=(r == R - 1)
                 )

@@ -14,62 +14,74 @@ FLOPS = 2 * K * M * V
 
 def tile_lookup_lse_relu_kernel(tc, tab, x0, w, b, offs, out):
     nc = tc.nc
-    with (
-        tc.tile_pool(name="held", bufs=1) as held,
-        tc.tile_pool(name="work", bufs=2) as work,
-        tc.psum_pool(name="psum", bufs=2) as psum,
-    ):
+    pieces = [(r, j) for j in range(0, V, C) for r in range(R)]
+    with tc.tile_pool(name="held", bufs=1) as held, tc.psum_pool(name="psum", bufs=1) as psum:
+
+        def tiles(kind):
+            return {(r, j): held.tile([P, C], F32, name=f"{kind}_{r}_{j}") for r, j in pieces}
+
         offsets = held.tile([P, D * V // 16], U16, name="offsets")
         nc.sync.dma_start(offsets[:], offs)
-
         tables = [held.tile([P, S], F32, name=f"table{r}") for r in range(R)]
-        own = {(r, j): held.tile([P, C], F32, name=f"own{r}_{j}") for j in range(0, V, C) for r in range(R)}
+        own = tiles("own")
+        for r, j in pieces:
+            rows = slice(r * P, (r + 1) * P)
+            if j == 0:
+                nc.sync.dma_start(tables[r][:], tab[rows, :])
+            nc.sync.dma_start(own[r, j][:], x0[rows, j : j + C])
         weights = held.tile([P, R * M], BF16, name="weights")
         bias = held.tile([P, 1], F32, name="bias")
-        identity = held.tile([P, P], F32, name="identity")
-        make_identity(nc, identity[:])
-        for j in range(0, V, C):
-            for r in range(R):
-                rows = slice(r * P, (r + 1) * P)
-                if j == 0:
-                    nc.sync.dma_start(tables[r][:], tab[rows, :])
-                nc.sync.dma_start(own[r, j][:], x0[rows, j : j + C])
         for r in range(R):
             nc.scalar.dma_start(weights[:, r * M : (r + 1) * M], w[r * P : (r + 1) * P, :])
         nc.scalar.dma_start(bias[:], b)
+        identity = held.tile([P, P], F32, name="identity")
+        make_identity(nc, identity[:])
 
-        def picked(r, d, j):
+        largest = [tiles(f"largest{d}") for d in range(D)]
+        diffs = [tiles(f"diff{t}") for t in range(1 + D)]
+        powers = [tiles(f"power{t}") for t in range(1 + D)]
+        sums = {(r, j): psum.tile([P, C], F32, name=f"sum_{r}_{j}") for r, j in pieces}
+        h = largest[D - 1]
+
+        def picked(r, j, d):
             first = (d * V + j) // 16
             return tables[r][:].indirect(offsets[:, first : first + C // 16])
 
+        def maximum(r, j, d):
+            before = own[r, j] if d == 0 else largest[d - 1][r, j]
+            nc.vector.tensor_tensor(largest[d][r, j][:], picked(r, j, d), before[:], Alu.max)
+
+        def exponential(r, j, t):
+            values = own[r, j][:] if t == 0 else picked(r, j, t - 1)
+            nc.vector.tensor_tensor(diffs[t][r, j][:], values, h[r, j][:], Alu.subtract)
+            nc.scalar.activation(powers[t][r, j][:], diffs[t][r, j][:], Act.Exp)
+            nc.tensor.matmul(sums[r, j][:], identity[:], powers[t][r, j][:], start=(t == 0), stop=(t == D))
+
+        logs = {}
+        for d in range(D):
+            maximum(*pieces[0], d)
+        exponential(*pieces[0], 0)
+        for i, (r, j) in enumerate(pieces):
+            following = pieces[i + 1 : i + 2]
+            for d in range(D):
+                exponential(r, j, 1 + d)
+                for piece in following:
+                    maximum(*piece, d)
+            if r == R - 1:
+                for q in range(R):
+                    logs[q, j] = diffs[D][R - 1 - q, j]
+                    nc.scalar.activation(logs[q, j][:], sums[q, j][:], Act.Ln)
+            for piece in following:
+                exponential(*piece, 0)
+
         for j in range(0, V, C):
-            h = [work.tile([P, C], F32, name=f"h{r}") for r in range(R)]
+            product = psum.tile([M, C], F32, name=f"product_{j}")
             for r in range(R):
-                part = work.tile([P, C], F32, name=f"part{r}")
-                nc.vector.tensor_tensor(part[:], picked(r, 0, j), own[r, j][:], Alu.max)
-                nc.vector.tensor_tensor(h[r][:], picked(r, 1, j), part[:], Alu.max)
-
-            sums = [psum.tile([P, C], F32, name=f"sum{r}") for r in range(R)]
-            for t in range(1 + D):
-                for r in range(R):
-                    diff = work.tile([P, C], F32, name=f"diff{r}")
-                    if t == 0:
-                        nc.vector.tensor_tensor(diff[:], own[r, j][:], h[r][:], Alu.subtract)
-                    else:
-                        nc.vector.tensor_tensor(diff[:], picked(r, t - 1, j), h[r][:], Alu.subtract)
-                    power = work.tile([P, C], F32, name=f"power{r}")
-                    nc.scalar.activation(power[:], diff[:], Act.Exp)
-                    nc.tensor.matmul(sums[r][:], identity[:], power[:], start=(t == 0), stop=(t == D))
-
-            product = psum.tile([M, C], F32, name="product")
-            for r in range(R):
-                log = work.tile([P, C], F32, name=f"log{r}")
-                nc.scalar.activation(log[:], sums[r][:], Act.Ln)
-                x = work.tile([P, C], BF16, name=f"x{r}")
-                nc.vector.tensor_tensor(x[:], h[r][:], log[:], Alu.add)
+                x = held.tile([P, C], BF16, name=f"x_{r}_{j}")
+                nc.vector.tensor_tensor(x[:], h[r, j][:], logs[r, j][:], Alu.add)
                 nc.tensor.matmul(
                     product[:], weights[:, r * M : (r + 1) * M], x[:], start=(r == 0), stop=(r == R - 1)
                 )
-            result = work.tile([M, C], F32, name="result")
-            nc.scalar.activation(result[:], product[:], Act.Relu, bias=bias[:])
+            result = held.tile([M, C], F32, name=f"result_{j}")
+            nc.vector.tensor_scalar(result[:], product[:], bias[:], 0.0, Alu.add, Alu.max)
             nc.sync.dma_start(out[:, j : j + C], result[:])

@@ -14,21 +14,21 @@ FLOPS = 2 * K * M * V
 
 def tile_lookup_lse_relu_kernel(tc, tab, x0, w, b, offs, out):
     nc = tc.nc
-    pieces = [(r, j) for j in range(0, V, C) for r in range(R)]
+    halves = range(0, V, C)
     with tc.tile_pool(name="held", bufs=1) as held, tc.psum_pool(name="psum", bufs=1) as psum:
 
         def tiles(kind):
-            return {(r, j): held.tile([P, C], F32, name=f"{kind}_{r}_{j}") for r, j in pieces}
+            return {(r, j): held.tile([P, C], F32, name=f"{kind}_{r}_{j}") for r in range(R) for j in halves}
 
         offsets = held.tile([P, D * V // 16], U16, name="offsets")
         nc.sync.dma_start(offsets[:], offs)
         tables = [held.tile([P, S], F32, name=f"table{r}") for r in range(R)]
         own = tiles("own")
-        for r, j in pieces:
+        for r in range(R):
             rows = slice(r * P, (r + 1) * P)
-            if j == 0:
-                nc.sync.dma_start(tables[r][:], tab[rows, :])
-            nc.sync.dma_start(own[r, j][:], x0[rows, j : j + C])
+            nc.sync.dma_start(tables[r][:], tab[rows, :])
+            for j in halves:
+                nc.sync.dma_start(own[r, j][:], x0[rows, j : j + C])
         weights = held.tile([P, R * M], BF16, name="weights")
         bias = held.tile([P, 1], F32, name="bias")
         for r in range(R):
@@ -38,50 +38,56 @@ def tile_lookup_lse_relu_kernel(tc, tab, x0, w, b, offs, out):
         make_identity(nc, identity[:])
 
         largest = [tiles(f"largest{d}") for d in range(D)]
+        h = largest[D - 1]
         diffs = [tiles(f"diff{t}") for t in range(1 + D)]
         powers = [tiles(f"power{t}") for t in range(1 + D)]
-        sums = {(r, j): psum.tile([P, C], F32, name=f"sum_{r}_{j}") for r, j in pieces}
-        h = largest[D - 1]
+        sums = {(r, j): psum.tile([P, C], F32, name=f"sum_{r}_{j}") for r in range(R) for j in halves}
 
-        def picked(r, j, d):
+        def picked(r, d, j):
             first = (d * V + j) // 16
             return tables[r][:].indirect(offsets[:, first : first + C // 16])
 
-        def maximum(r, j, d):
-            before = own[r, j] if d == 0 else largest[d - 1][r, j]
-            nc.vector.tensor_tensor(largest[d][r, j][:], picked(r, j, d), before[:], Alu.max)
+        def maximum(r, d):
+            before = own if d == 0 else largest[d - 1]
+            for j in halves:
+                nc.vector.tensor_tensor(largest[d][r, j][:], picked(r, d, j), before[r, j][:], Alu.max)
 
-        def exponential(r, j, t):
-            values = own[r, j][:] if t == 0 else picked(r, j, t - 1)
-            nc.vector.tensor_tensor(diffs[t][r, j][:], values, h[r, j][:], Alu.subtract)
-            nc.scalar.activation(powers[t][r, j][:], diffs[t][r, j][:], Act.Exp)
-            nc.tensor.matmul(sums[r, j][:], identity[:], powers[t][r, j][:], start=(t == 0), stop=(t == D))
+        def exponential(r, t):
+            for j in halves:
+                values = own[r, j][:] if t == 0 else picked(r, t - 1, j)
+                diff, power = diffs[t][r, j], powers[t][r, j]
+                nc.vector.tensor_tensor(diff[:], values, h[r, j][:], Alu.subtract)
+                nc.scalar.activation(power[:], diff[:], Act.Exp)
+                nc.tensor.matmul(sums[r, j][:], identity[:], power[:], start=(t == 0), stop=(t == D))
 
-        logs = {}
         for d in range(D):
-            maximum(*pieces[0], d)
-        exponential(*pieces[0], 0)
-        for i, (r, j) in enumerate(pieces):
-            following = pieces[i + 1 : i + 2]
-            for d in range(D):
-                exponential(r, j, 1 + d)
-                for piece in following:
-                    maximum(*piece, d)
-            if r == R - 1:
-                for q in range(R):
-                    logs[q, j] = diffs[D][R - 1 - q, j]
-                    nc.scalar.activation(logs[q, j][:], sums[q, j][:], Act.Ln)
-            for piece in following:
-                exponential(*piece, 0)
+            maximum(0, d)
+        exponential(0, 0)
+        for d in range(D):
+            exponential(0, 1 + d)
+            maximum(1, d)
+        for t in range(1 + D):
+            exponential(1, t)
 
-        for j in range(0, V, C):
-            product = psum.tile([M, C], F32, name=f"product_{j}")
+        logs = {(0, 0): diffs[D][1, C], (0, C): powers[D][1, C]}
+        for j in halves:
+            logs[1, j] = held.tile([P, C], F32, name=f"log_1_{j}")
+        x = {(r, j): held.tile([P, C], BF16, name=f"x_{r}_{j}") for r in range(R) for j in halves}
+        quarters = [(j, slice(c, c + C // 2)) for j in halves for c in range(0, C, C // 2)]
+        for j, cols in quarters:
             for r in range(R):
-                x = held.tile([P, C], BF16, name=f"x_{r}_{j}")
-                nc.vector.tensor_tensor(x[:], h[r, j][:], logs[r, j][:], Alu.add)
+                nc.scalar.activation(logs[r, j][:, cols], sums[r, j][:, cols], Act.Ln)
+        products = {j: psum.tile([M, C], F32, name=f"product_{j}") for j in halves}
+        for j, cols in quarters:
+            for r in range(R):
+                nc.vector.tensor_tensor(x[r, j][:, cols], h[r, j][:, cols], logs[r, j][:, cols], Alu.add)
                 nc.tensor.matmul(
-                    product[:], weights[:, r * M : (r + 1) * M], x[:], start=(r == 0), stop=(r == R - 1)
+                    products[j][:, cols],
+                    weights[:, r * M : (r + 1) * M],
+                    x[r, j][:, cols],
+                    start=(r == 0),
+                    stop=(r == R - 1),
                 )
-            result = held.tile([M, C], F32, name=f"result_{j}")
-            nc.vector.tensor_scalar(result[:], product[:], bias[:], 0.0, Alu.add, Alu.max)
-            nc.sync.dma_start(out[:, j : j + C], result[:])
+            result = held.tile([M, C // 2], F32, name=f"result_{j}_{cols.start}")
+            nc.scalar.activation(result[:], products[j][:, cols], Act.Relu, bias=bias[:])
+            nc.sync.dma_start(out[:, j + cols.start : j + cols.stop], result[:])

import concourse.mybir as mybir
from concourse.masks import make_identity

F32, BF16, U16 = mybir.dt.float32, mybir.dt.bfloat16, mybir.dt.uint16
Alu = mybir.AluOpType
Act = mybir.ActivationFunctionType

P = 128
K, S, D, V, M = 256, 2048, 2, 1024, 128
R = K // P
C = 512
FLOPS = 2 * K * M * V


def tile_lookup_lse_relu_kernel(tc, tab, x0, w, b, offs, out):
    nc = tc.nc
    halves = range(0, V, C)
    with tc.tile_pool(name="held", bufs=1) as held, tc.psum_pool(name="psum", bufs=1) as psum:

        def tiles(kind):
            return {(r, j): held.tile([P, C], F32, name=f"{kind}_{r}_{j}") for r in range(R) for j in halves}

        offsets = held.tile([P, D * V // 16], U16, name="offsets")
        nc.sync.dma_start(offsets[:], offs)
        tables = [held.tile([P, S], F32, name=f"table{r}") for r in range(R)]
        own = tiles("own")
        for r in range(R):
            rows = slice(r * P, (r + 1) * P)
            nc.sync.dma_start(tables[r][:], tab[rows, :])
            for j in halves:
                nc.sync.dma_start(own[r, j][:], x0[rows, j : j + C])
        weights = held.tile([P, R * M], BF16, name="weights")
        bias = held.tile([P, 1], F32, name="bias")
        for r in range(R):
            nc.scalar.dma_start(weights[:, r * M : (r + 1) * M], w[r * P : (r + 1) * P, :])
        nc.scalar.dma_start(bias[:], b)
        identity = held.tile([P, P], F32, name="identity")
        make_identity(nc, identity[:])

        largest = [tiles(f"largest{d}") for d in range(D)]
        h = largest[D - 1]
        diffs = [tiles(f"diff{t}") for t in range(1 + D)]
        powers = [tiles(f"power{t}") for t in range(1 + D)]
        sums = {(r, j): psum.tile([P, C], F32, name=f"sum_{r}_{j}") for r in range(R) for j in halves}

        def picked(r, d, j):
            first = (d * V + j) // 16
            return tables[r][:].indirect(offsets[:, first : first + C // 16])

        def maximum(r, d):
            before = own if d == 0 else largest[d - 1]
            for j in halves:
                nc.vector.tensor_tensor(largest[d][r, j][:], picked(r, d, j), before[r, j][:], Alu.max)

        def exponential(r, t):
            for j in halves:
                values = own[r, j][:] if t == 0 else picked(r, t - 1, j)
                diff, power = diffs[t][r, j], powers[t][r, j]
                nc.vector.tensor_tensor(diff[:], values, h[r, j][:], Alu.subtract)
                nc.scalar.activation(power[:], diff[:], Act.Exp)
                nc.tensor.matmul(sums[r, j][:], identity[:], power[:], start=(t == 0), stop=(t == D))

        for d in range(D):
            maximum(0, d)
        exponential(0, 0)
        for d in range(D):
            exponential(0, 1 + d)
            maximum(1, d)
        for t in range(1 + D):
            exponential(1, t)

        logs = {(0, 0): diffs[D][1, C], (0, C): powers[D][1, C]}
        for j in halves:
            logs[1, j] = held.tile([P, C], F32, name=f"log_1_{j}")
        x = {(r, j): held.tile([P, C], BF16, name=f"x_{r}_{j}") for r in range(R) for j in halves}
        quarters = [(j, slice(c, c + C // 2)) for j in halves for c in range(0, C, C // 2)]
        for j, cols in quarters:
            for r in range(R):
                nc.scalar.activation(logs[r, j][:, cols], sums[r, j][:, cols], Act.Ln)
        products = {j: psum.tile([M, C], F32, name=f"product_{j}") for j in halves}
        for j, cols in quarters:
            for r in range(R):
                nc.vector.tensor_tensor(x[r, j][:, cols], h[r, j][:, cols], logs[r, j][:, cols], Alu.add)
                nc.tensor.matmul(
                    products[j][:, cols],
                    weights[:, r * M : (r + 1) * M],
                    x[r, j][:, cols],
                    start=(r == 0),
                    stop=(r == R - 1),
                )
            result = held.tile([M, C // 2], F32, name=f"result_{j}_{cols.start}")
            nc.scalar.activation(result[:], products[j][:, cols], Act.Relu, bias=bias[:])
            nc.sync.dma_start(out[:, j + cols.start : j + cols.stop], result[:])
